import numpy as np, ml_dtypes
CORES = [76,84,92,100,108,116,124]
N = 7
DEG, TK = 4, 128
MASK = [[1,3,4,0],[1,3,4,0],[1,3,4,2],[1,3,4,0],[1,3,4,0],[1,3,4,5],[1,3,4,6]]
def setup_inputs(rng):
    return {"x": rng.standard_normal((N, 128, TK), dtype=np.float32).astype(ml_dtypes.bfloat16), "w": rng.standard_normal((N, 128, DEG * 128), dtype=np.float32).astype(ml_dtypes.bfloat16)}
def setup_inputs_big(rng):
    d = setup_inputs(rng)
    for k in ("x", "w"): d[k] = (d[k].astype(np.float32) * 1024.0).astype(d[k].dtype)
    return d
def setup_inputs_small(rng):
    d = setup_inputs(rng)
    for k in ("x", "w"): d[k] = (d[k].astype(np.float32) * (1 / 1024.0)).astype(d[k].dtype)
    return d
def setup_inputs_apart(rng):
    d = setup_inputs(rng)
    f = (10.0 ** rng.permutation(np.linspace(-1.5, 1.5, N))).astype(np.float32).reshape(N, 1, 1)
    for k in ("x", "w"): d[k] = (d[k].astype(np.float32) * f).astype(d[k].dtype)
    return d
def reference(x, w):
    X, W = x.astype(np.float64), w.astype(np.float64)
    y = np.zeros((N, 128, TK))
    for r in range(N):
        for i, j in enumerate(MASK[r]):
            y[r] += W[r][:, 128 * i:128 * i + 128].T @ X[j]
    return {"y": y.astype(ml_dtypes.bfloat16 if x.dtype != np.float64 else np.float64)}

from concourse.bass import DstId, RemoteDMATransfer

TK = 128
DEG = 4
NRANKS = 7
DIRECT = 2
K_STAGE1 = 8
K_OFF = 8

SCRATCH = {
    "xs": ("dram", [128, TK], "bfloat16"),
    "xin": ("sbuf", [128, DEG * TK], "bfloat16"),
    "wsb": ("sbuf", [128, DEG * TK], "bfloat16"),
    "acc": ("psum", [128, TK], "float32"),
    "ysb": ("sbuf", [128, TK], "bfloat16"),
}
SEMAPHORES = ["ld", "lx", "lw", "hin", "snt", "mm", "cp", "st"] + ["a%d" % j for j in range(NRANKS)]


def _bits(mask):
    return [b for b in range(mask.bit_length()) if (mask >> b) & 1]


def _pick(mask, n, avoid=0):
    order = [b for b in _bits(mask) if not (avoid >> b) & 1] + [b for b in _bits(mask) if (avoid >> b) & 1]
    m = 0
    for b in order[:n]:
        m |= 1 << b
    return m


def _plan(T, topo):
    cores, mask = T.cores, T.tables["MASK"]
    n = len(cores)
    everyone = range(topo.CHIPS * topo.CORES_PER_CHIP)
    used = set(cores)
    load = {}
    plan = {}
    for j in range(n):
        s = cores[j]
        needs = [r for r in range(n) if r != j and j in mask[r]]
        if not needs:
            continue
        near = [r for r in needs if topo.may_write(s, cores[r])]
        far = [r for r in needs if not topo.may_write(s, cores[r])]
        far.sort(key=lambda r: topo.mates(topo.chip(s), topo.chip(cores[r])))
        relays = []
        for r in far + near[DIRECT:]:
            d = cores[r]
            cand = [h for h in everyone if topo.chip(h) == topo.chip(s) and h not in used and topo.may_write(h, d)]
            h = min(cand, key=lambda c: (load.get(("out", topo.chip(s), topo.die(c)), 0)
                                         + load.get(("in", topo.chip(d), topo.die(c)), 0),
                                         topo.die(c) != topo.die(s), c))
            used.add(h)
            for k in (("out", topo.chip(s), topo.die(h)), ("in", topo.chip(d), topo.die(h))):
                load[k] = load.get(k, 0) + 1
            relays.append((h, r))
        plan[j] = (near[:DIRECT], relays)
    return plan


def _slot(T, r, j):
    i = T.tables["MASK"][r].index(j)
    return T.xin[:, i * TK:(i + 1) * TK]


def _send(g, T, topo, src, dests, mask, remote_sem):
    ids = []
    for c, _ in dests:
        rid, pid, _se = topo.addr(c)
        ids.append(DstId(rid=rid, pnc=pid))
    g.remote_dma_fused([RemoteDMATransfer(dst_ids=ids, dma_engine_mask=mask, remote_sem=remote_sem,
                                          srcs=[src], dsts=[ap for _, ap in dests])], local_sem=T.sem.snt)
    return len(_bits(mask))


def rank_program(g, core, T, topo):
    plan = _plan(T, topo)
    cores, table = T.cores, T.tables["MASK"]
    rank = T.rank_of(core)

    if rank is None:
        for j, (_direct, relays) in plan.items():
            for h, r in relays:
                if h != core:
                    continue
                d = cores[r]
                rid, pid, _se = topo.addr(d)
                m = _pick(topo.mask(core, d), K_OFF)
                g.wait_ge(T.sem.hin, K_STAGE1)
                g.remote_dma(out_ap=_slot(T, r, j), in_ap=T.xs[:], remote_sem=T.sem["a%d" % j], local_sem=T.sem.snt,
                             pid=pid, routing_id=rid, dma_engine_mask=m)
                g.wait_ge(T.sem.snt, len(_bits(m)))
        return

    own = table[rank].index(rank) if rank in table[rank] else None
    source = rank in plan

    if source:
        g.sync.dma_start(T.xs[:], T.x[:]).then_inc(T.sem.ld, 16)
    if own is not None:
        g.sync.dma_start(T.xin[:, own * TK:(own + 1) * TK], T.x[:]).then_inc(T.sem.lx, 16)
    (g.sync if source else g.scalar).dma_start(T.wsb[:], T.w[:]).then_inc(T.sem.lw, 16)

    if source:
        direct, relays = plan[rank]
        off = 0
        for r in direct:
            off |= topo.mask(core, cores[r])
        sent = 0
        g.wait_ge(T.sem.ld, 16)
        if relays:
            on = topo.mask(core, relays[0][0])
            sent += _send(g, T, topo, T.xs[:], [(h, T.xs[:]) for h, _ in relays], _pick(on, K_STAGE1, avoid=off),
                          T.sem.hin)
        if direct:
            sent += _send(g, T, topo, T.xs[:], [(cores[r], _slot(T, r, rank)) for r in direct], _pick(off, K_OFF),
                          T.sem["a%d" % rank])
        g.wait_ge(T.sem.snt, sent)

    def when(i):
        j = table[rank][i]
        if j == rank:
            return (0, 0)
        direct, relays = plan[j]
        if rank in direct:
            return (1, direct.index(rank))
        return (2, [r for _, r in relays].index(rank))

    order = sorted(range(DEG), key=when)
    g.tensor.wait_ge(T.sem.lw, 16)
    for n, i in enumerate(order):
        j = table[rank][i]
        if j == rank:
            g.tensor.wait_ge(T.sem.lx, 16)
        else:
            g.tensor.wait_ge(T.sem["a%d" % j], K_OFF)
        mm = g.tensor.matmul(T.acc[:], T.wsb[:, i * TK:(i + 1) * TK], T.xin[:, i * TK:(i + 1) * TK],
                             start=(n == 0), stop=(n == DEG - 1))
    mm.then_inc(T.sem.mm, 1)

    g.vector.wait_ge(T.sem.mm, 1)
    g.vector.tensor_copy(T.ysb[:], T.acc[:]).then_inc(T.sem.cp, 1)
    g.scalar.wait_ge(T.sem.cp, 1)
    g.scalar.dma_start(T.y[:], T.ysb[:]).then_inc(T.sem.st, 16)
    g.scalar.wait_ge(T.sem.st, 16)
